import numpy as np
import ml_dtypes


def mxq(x, axis, fmt="e4m3"):
    dtype, down = {"e4m3": (ml_dtypes.float8_e4m3fn, 7), "e5m2": (ml_dtypes.float8_e5m2, 14)}[fmt]
    v = np.moveaxis(np.asarray(x, np.float32).astype(ml_dtypes.bfloat16).astype(np.float64), axis, -1)
    blocks = v.reshape(v.shape[:-1] + (-1, 32))
    amax = np.abs(blocks).max(-1, keepdims=True)
    byte = np.maximum(np.where(amax > 0, np.frexp(amax)[1] - 1 + 127, 0) - down, 1)
    scale = np.exp2(byte - 127.0)
    codes = (blocks / scale).astype(np.float32).astype(dtype).astype(np.float64)
    return np.moveaxis((codes * scale).reshape(v.shape), -1, axis)


WIDE = False


def mx_kscale(k):
    if not WIDE:
        return np.ones(k)
    levels = np.array([10, -10, 5, -5, 0])
    if k % 512:
        return np.exp2(np.random.permutation(np.resize(levels, k // 32))).repeat(32)
    a = np.empty((k // 512, 16))
    for p in range(k // 512):
        a[p, :8] = np.random.permutation(np.resize(levels, 8))
        for g in range(8):
            far = levels[np.abs(levels - a[p, g]) >= 10]
            a[p, g + 8] = far[np.random.randint(len(far))]
    return np.exp2(a.ravel()).repeat(32)


def f64(x):
    return np.asarray(x).astype(np.float64)


def striped(idx):
    return np.tile(idx.reshape(-1, 16).T, (8, 1)).astype(np.uint16)


def unstriped(offs):
    return offs[:16].T.reshape(-1).astype(np.int64)


def pack_weight(w):
    k, n = w.shape
    w = f64(np.asarray(w, np.float32).astype(ml_dtypes.bfloat16)).reshape(k // 32, 32, n)
    amax = np.abs(w).max(1)
    byte = np.clip(np.where(amax > 0, np.frexp(amax)[1] - 1 + 127 - 7, 1), 1, 254)
    scaled = (w * np.exp2(127.0 - byte)[:, None, :]).reshape(k, n).astype(np.float32)
    words = np.ascontiguousarray(scaled.reshape(k // 512, 128, 4, n).transpose(0, 1, 3, 2)).astype(ml_dtypes.float8_e4m3fn).view(np.uint8)
    return words, np.ascontiguousarray(byte.astype(np.uint8).reshape(k // 512, 16, n))


def unpack_weight(words, scales):
    g, p, n, _ = words.shape
    vals = np.ascontiguousarray(words).view(ml_dtypes.float8_e4m3fn).astype(np.float64) * np.repeat(np.exp2(scales.astype(np.float64) - 127.0), 8, axis=1)[..., None]
    return vals.transpose(0, 1, 3, 2).reshape(g * 512, n)


def planes(y):
    n, m = y.shape
    v = y.astype(np.float32).astype(ml_dtypes.bfloat16).astype(np.float64).reshape(n // 32, 32, m)
    top = np.abs(v).max(1)
    byte = np.clip(np.where(top > 0, np.frexp(top)[1] - 1 + 127 - 7, 1), 1, 254)
    codes = (v * np.exp2(127.0 - byte)[:, None, :]).reshape(n, m).astype(np.float32).astype(ml_dtypes.float8_e4m3fn).view(np.uint8)
    words = codes.reshape(n // 512, 128, 4, m).transpose(0, 1, 3, 2)
    return np.ascontiguousarray(words), np.ascontiguousarray(byte.astype(np.uint8).reshape(n // 512, 16, m))


K, T, S, H, N = 1024, 4096, 1024, 512, 512


def setup_inputs():
    n = np.random.standard_normal
    s = mx_kscale(K)[:, None]
    u = mx_kscale(H)
    packed_xT = pack_weight(n((K, T)) * s)
    return {
        "x_words": packed_xT[0],
        "x_scales": packed_xT[1],
        "w1": (n((K, N)) / np.sqrt(K) / s).astype(np.float32),
        "w2": (n((K, N)) / np.sqrt(K) / s).astype(np.float32),
        "w3": (n((K, H)) / np.sqrt(K) / s * u).astype(np.float32),
        "w4": (n((H, N)) / np.sqrt(H) / u[:, None]).astype(np.float32),
        "offs": striped(np.random.permutation(T)[:S]),
    }


def reference(x_words, x_scales, w1, w2, w3, w4, offs):
    xq = unpack_weight(x_words, x_scales)[:, unstriped(offs)]
    y = mxq(f64(w1), 0, "e4m3").T @ xq
    ex = np.exp(y - y.max(axis=1, keepdims=True))
    a = ex / ex.sum(axis=1, keepdims=True)
    p = a * ((mxq(f64(w2), 0, "e4m3").T @ xq))
    gg = p.sum(axis=1, keepdims=True)
    z = ((mxq(f64(w3), 0, "e4m3").T @ xq)) * gg
    out_0 = mxq(f64(w4), 0, "e4m3").T @ mxq(z, 0, "e4m3")
    return (out_0,) + planes(out_0)

@@ -1,0 +1,292 @@
+from contextlib import ExitStack
+
+import concourse.mybir as mybir
+
+K, T, S, H, N = 1024, 4096, 1024, 512, 512
+FLOPS = 2 * S * (3 * K * N + H * N)
+
+F32 = mybir.dt.float32
+BF16 = mybir.dt.bfloat16
+I32 = mybir.dt.int32
+U32 = mybir.dt.uint32
+U16 = mybir.dt.uint16
+U8 = mybir.dt.uint8
+FP8X4 = mybir.dt.float8_e4m3fn_x4
+ALU = mybir.AluOpType
+ACT = mybir.ActivationFunctionType
+
+P = 128
+PACK = 4
+K_PASS = P * PACK
+PASSES = K // K_PASS
+BANK = 512
+HALVES = S // BANK
+CHUNK = 128
+CHUNKS = S // CHUNK
+CAST_ON = {"w1": "ssvs", "w2": "ssvs", "w3": "ssvs", "w4": "ss"}
+ROUND_ON_VECTOR_FROM = 4
+
+
+def tile_picked_yfastf_none_po_kernel(
+    tc, x_words, x_scales, w1, w2, w3, w4, offs, out_0, out_1, out_2
+):
+    nc = tc.nc
+    with ExitStack() as ctx:
+        keep = ctx.enter_context(tc.tile_pool(name="keep", bufs=1))
+        late = ctx.enter_context(tc.tile_pool(name="late", bufs=1))
+        psum = ctx.enter_context(tc.psum_pool(name="psum", bufs=1))
+        banks = [psum.tile([P, BANK], F32, name=f"bank{b}") for b in range(8)]
+
+        def sbuf(name, shape, dtype):
+            return keep.tile(shape, dtype, name=name, align_bytes=64)
+
+        offsets = keep.tile([P, S // 16], U16, name="offsets")
+        nc.sync.dma_start(offsets[:], offs)
+
+        scale_table = sbuf("scale_table", [P, T], U8)
+        nc.vector.memset(scale_table[:].bitcast(I32), 0)
+
+        warm = late.tile([P, T + 7 * PACK * N], F32, name="warm", offset=0)
+        nc.vector.memset(warm[:, 0:1], 0.0)
+        nc.scalar.activation(out=warm[:, 1:2], in_=warm[:, 0:1], func=ACT.Exp)
+
+        word_table = [sbuf("word_table0", [P, T], U32), late.tile([P, T], U32, name="word_table1", offset=0)]
+        weights = {"w1": w1, "w2": w2, "w3": w3, "w4": w4}
+        raw = {}
+
+        def load_words(g):
+            nc.sync.dma_start(
+                out=word_table[g][:].bitcast(I32),
+                in_=x_words[g].rearrange("p n t -> p (n t)").bitcast(I32),
+            )
+
+        def load_scales(g):
+            for q in range(4):
+                nc.sync.dma_start(
+                    out=scale_table[32 * q + PACK * g : 32 * q + PACK * (g + 1), :].bitcast(I32),
+                    in_=x_scales[g, 4 * q : 4 * q + 4, :].bitcast(I32),
+                )
+
+        def load_weight(name, g):
+            place = 4 * (T + len(raw) * PACK * N)
+            raw[name, g] = late.tile([P, PACK, N], F32, name=f"raw_{name}_{g}", offset=place)
+            rows = weights[name][g * K_PASS : (g + 1) * K_PASS, :]
+            nc.sync.dma_start(out=raw[name, g][:], in_=rows.rearrange("(p j) c -> p j c", j=PACK))
+
+        load_words(0)
+        load_scales(0)
+        load_weight("w1", 0)
+        load_scales(1)
+        load_words(1)
+        load_weight("w1", 1)
+        for name in ("w2", "w3"):
+            for g in range(PASSES):
+                load_weight(name, g)
+        load_weight("w4", 0)
+
+        rounded, w_codes, w_scales = {}, {}, {}
+
+        def cast_weight(name, g, u):
+            rounded[name, g, u] = sbuf(f"rounded_{name}_{g}_{u}", [P, 2 * P * PACK], BF16)
+            dst = rounded[name, g, u][:].rearrange("p (t m j) -> p m t j", t=2, j=PACK)
+            src = raw[name, g][:].rearrange("p j (m t) -> p m t j", t=PACK)[:, :, 2 * u : 2 * u + 2, :]
+            where = CAST_ON[name][2 * g + u]
+            if where == "s":
+                nc.scalar.copy(out=dst, in_=src)
+            elif where == "v":
+                nc.vector.tensor_copy(out=dst, in_=src)
+            else:
+                nc.gpsimd.tensor_scalar(out=dst, in0=src, scalar1=1.0, scalar2=0.0, op0=ALU.mult, op1=ALU.add)
+
+        def quantise_weight(name, g, u):
+            w_codes[name, g, u] = sbuf(f"codes_{name}_{g}_{u}", [P, 2 * P], U32)
+            w_scales[name, g, u] = sbuf(f"scales_{name}_{g}_{u}", [P, 2 * P], U8)
+            nc.vector.quantize_mx(
+                out=w_codes[name, g, u][:].bitcast(FP8X4), scales=w_scales[name, g, u][:], in_=rounded[name, g, u][:]
+            )
+
+        def stationary(name, g, t):
+            cols = slice((t % 2) * P, (t % 2 + 1) * P)
+            return w_codes[name, g, t // 2][:, cols].bitcast(FP8X4), w_scales[name, g, t // 2][:, cols]
+
+        x_scale = sbuf("x_scale", [P, S], U8)
+        x_codes = [sbuf(f"x_codes{g}", [P, S], U32) for g in range(PASSES)]
+
+        def gather_words(g, h):
+            nc.vector.tensor_copy(
+                out=x_codes[g][:, h * BANK : (h + 1) * BANK],
+                in_=word_table[g][:].indirect(offsets[:, h * BANK // 16 : (h + 1) * BANK // 16]),
+            )
+
+        def project(out, name, g, t, cols):
+            codes, scales = stationary(name, g, t)
+            nc.tensor.matmul_mx(
+                out=out,
+                lhsT=codes,
+                lhsT_scale=scales,
+                rhs=x_codes[g][:, cols].bitcast(FP8X4),
+                rhs_scale=x_scale[PACK * g : P, cols],
+                start=(g == 0),
+                stop=(g == PASSES - 1),
+            )
+
+        def project_wide(name, g, t):
+            for h in range(HALVES):
+                project(banks[HALVES * t + h][:], name, g, t, slice(h * BANK, (h + 1) * BANK))
+
+        for g in range(PASSES):
+            for h in range(HALVES):
+                gather_words(g, h)
+            if g == 0:
+                nc.vector.tensor_copy(out=x_scale[:], in_=scale_table[:].indirect(offsets[:]))
+            for u in range(2):
+                cast_weight("w1", g, u)
+            for u in range(2):
+                quantise_weight("w1", g, u)
+            for t in range(PACK):
+                project_wide("w1", g, t)
+
+        neg_y = [sbuf(f"neg_y{t}", [P, S], F32) for t in range(PACK)]
+        ex = [sbuf(f"ex{t}", [P, S], F32) for t in range(PACK)]
+        neg_max = [sbuf(f"neg_max{t}", [P, HALVES], F32) for t in range(PACK)]
+        total = [sbuf(f"total{t}", [P, 1], F32) for t in range(PACK)]
+        inverse = [sbuf(f"inverse{t}", [P, 1], F32) for t in range(PACK)]
+        part = sbuf("part", [P, HALVES, PACK], F32)
+        gg = sbuf("gg", [P, PACK], F32)
+
+        def negate_and_min(t, h):
+            nc.vector.tensor_scalar(
+                out=neg_y[t][:, h * BANK : (h + 1) * BANK],
+                in0=banks[HALVES * t + h][:],
+                scalar1=-1.0,
+                scalar2=None if h == 0 else neg_max[t][:, h - 1 : h],
+                op0=ALU.mult,
+                op1=ALU.min,
+                accum_out=neg_max[t][:, h : h + 1],
+            )
+
+        def exponentiate(t):
+            nc.scalar.activation(
+                out=ex[t][:],
+                in_=neg_y[t][:],
+                func=ACT.Exp,
+                scale=-1.0,
+                bias=neg_max[t][:, HALVES - 1 : HALVES],
+                accum_out=total[t][:],
+            )
+
+        def weigh(t, h):
+            cols = slice(h * BANK, (h + 1) * BANK)
+            nc.vector.scalar_tensor_tensor(
+                out=neg_y[t][:, cols],
+                in0=banks[HALVES * t + h][:],
+                scalar=inverse[t][:],
+                in1=ex[t][:, cols],
+                op0=ALU.mult,
+                op1=ALU.mult,
+                accum_out=part[:, h, t : t + 1],
+            )
+
+        for u in range(2):
+            cast_weight("w2", 0, u)
+        for u in range(2):
+            for h in range(HALVES):
+                for t in (2 * u, 2 * u + 1):
+                    negate_and_min(t, h)
+        exponentiate(0)
+        for u in range(2):
+            cast_weight("w2", 1, u)
+        for t in range(1, PACK):
+            exponentiate(t)
+        for u in range(2):
+            for g in range(PASSES):
+                quantise_weight("w2", g, u)
+        for t in range(PACK):
+            nc.vector.reciprocal(out=inverse[t][:], in_=total[t][:])
+        for t in range(PACK):
+            for g in range(PASSES):
+                project_wide("w2", g, t)
+        for g in range(PASSES):
+            for u in range(2):
+                cast_weight("w3", g, u)
+        for t in range(PACK):
+            for h in range(HALVES):
+                weigh(t, h)
+            if t >= 2:
+                for u in range(2):
+                    quantise_weight("w3", t - 2, u)
+        for u in range(2):
+            cast_weight("w4", 0, u)
+        nc.vector.tensor_tensor(out=gg[:], in0=part[:, 0, :], in1=part[:, 1, :], op=ALU.add)
+        for u in range(2):
+            quantise_weight("w4", 0, u)
+
+        for c in range(CHUNKS):
+            for t in range(PACK):
+                for g in range(PASSES):
+                    project(banks[c][:, t * CHUNK : (t + 1) * CHUNK], "w3", g, t, slice(c * CHUNK, (c + 1) * CHUNK))
+
+        z = [sbuf(f"z{c}", [P, CHUNK * PACK], BF16) for c in range(CHUNKS)]
+        z_codes = [sbuf(f"z_codes{c}", [P, CHUNK], U32) for c in range(CHUNKS)]
+        z_scales = [sbuf(f"z_scales{c}", [P, CHUNK], U8) for c in range(CHUNKS)]
+        result = [sbuf(f"result{c}", [P, PACK, 2 * CHUNK], F32) for c in range(CHUNKS // 2)]
+        result_bf = [sbuf(f"result_bf{c}", [P, CHUNK * PACK], BF16) for c in range(CHUNKS)]
+        out_codes = sbuf("out_codes", [P, S], U32)
+        out_scales = sbuf("out_scales", [P, S], U8)
+        out_rows = out_0.rearrange("(p t) j -> p t j", t=PACK)
+        out_words = out_1[0].rearrange("p n t -> p (n t)").bitcast(I32)
+
+        def scale_hidden(c):
+            nc.vector.tensor_tensor(
+                out=z[c][:].rearrange("p (n t) -> p n t", t=PACK),
+                in0=banks[c][:].rearrange("p (t n) -> p n t", t=PACK),
+                in1=gg[:].unsqueeze(1).to_broadcast([P, CHUNK, PACK]),
+                op=ALU.mult,
+            )
+
+        def output_layer(c):
+            nc.vector.quantize_mx(out=z_codes[c][:].bitcast(FP8X4), scales=z_scales[c][:], in_=z[c][:])
+            for t in range(PACK):
+                codes, scales = stationary("w4", 0, t)
+                nc.tensor.matmul_mx(
+                    out=banks[c][:, t * CHUNK : (t + 1) * CHUNK],
+                    lhsT=codes,
+                    lhsT_scale=scales,
+                    rhs=z_codes[c][:].bitcast(FP8X4),
+                    rhs_scale=z_scales[c][:],
+                    start=True,
+                    stop=True,
+                )
+
+        def leave_psum(c):
+            mine = result[c // 2][:, :, (c % 2) * CHUNK : (c % 2 + 1) * CHUNK]
+            nc.scalar.copy(out=mine, in_=banks[c][:].rearrange("p (t n) -> p t n", t=PACK))
+            dst = result_bf[c][:].rearrange("p (n t) -> p n t", t=PACK)
+            if c >= ROUND_ON_VECTOR_FROM:
+                nc.vector.tensor_copy(out=dst, in_=mine.rearrange("p t n -> p n t"))
+            else:
+                nc.scalar.copy(out=dst, in_=banks[c][:].rearrange("p (t n) -> p n t", t=PACK))
+
+        def hand_out(c):
+            cols = slice(c * CHUNK, (c + 1) * CHUNK)
+            nc.vector.quantize_mx(out=out_codes[:, cols].bitcast(FP8X4), scales=out_scales[:, cols], in_=result_bf[c][:])
+            if c % 2 == 1:
+                pair = slice((c - 1) * CHUNK, (c + 1) * CHUNK)
+                nc.sync.dma_start(out=out_rows[:, :, pair], in_=result[c // 2][:])
+                nc.sync.dma_start(out=out_words[:, pair], in_=out_codes[:, pair].bitcast(I32))
+
+        for step in range(CHUNKS + 3):
+            if step < CHUNKS:
+                scale_hidden(step)
+            if 0 <= step - 1 < CHUNKS:
+                output_layer(step - 1)
+            if 0 <= step - 2 < CHUNKS:
+                leave_psum(step - 2)
+            if 0 <= step - 3 < CHUNKS:
+                hand_out(step - 3)
+        for q in range(4):
+            queue = nc.scalar if q % 2 else nc.sync
+            queue.dma_start(
+                out=out_2[0, 4 * q : 4 * q + 4, :].bitcast(I32),
+                in_=out_scales[32 * q : 32 * q + 4, :].bitcast(I32),
+            )

@@ -23,8 +23,10 @@ BANK = 512
 HALVES = S // BANK
 CHUNK = 128
 CHUNKS = S // CHUNK
-CAST_ON = {"w1": "ssvs", "w2": "ssvs", "w3": "ssvs", "w4": "ss"}
-ROUND_ON_VECTOR_FROM = 4
+CAST_ON = {"w1": "ssvs", "w2": "ssvs", "w3": "ssvv"}
+HIDDEN_AHEAD = 3
+W3_AFTER = 1
+ROUND_ON_VECTOR_FROM = 3
 
 
 def tile_picked_yfastf_none_po_kernel(
@@ -34,6 +36,7 @@ def tile_picked_yfastf_none_po_kernel(
     with ExitStack() as ctx:
         keep = ctx.enter_context(tc.tile_pool(name="keep", bufs=1))
         late = ctx.enter_context(tc.tile_pool(name="late", bufs=1))
+        reuse = ctx.enter_context(tc.tile_pool(name="reuse", bufs=1))
         psum = ctx.enter_context(tc.psum_pool(name="psum", bufs=1))
         banks = [psum.tile([P, BANK], F32, name=f"bank{b}") for b in range(8)]
 
@@ -43,7 +46,7 @@ def tile_picked_yfastf_none_po_kernel(
         offsets = keep.tile([P, S // 16], U16, name="offsets")
         nc.sync.dma_start(offsets[:], offs)
 
-        scale_table = sbuf("scale_table", [P, T], U8)
+        scale_table = reuse.tile([P, T], U8, name="scale_table", offset=0, align_bytes=64)
         nc.vector.memset(scale_table[:].bitcast(I32), 0)
 
         warm = late.tile([P, T + 7 * PACK * N], F32, name="warm", offset=0)
@@ -71,7 +74,12 @@ def tile_picked_yfastf_none_po_kernel(
             place = 4 * (T + len(raw) * PACK * N)
             raw[name, g] = late.tile([P, PACK, N], F32, name=f"raw_{name}_{g}", offset=place)
             rows = weights[name][g * K_PASS : (g + 1) * K_PASS, :]
-            nc.sync.dma_start(out=raw[name, g][:], in_=rows.rearrange("(p j) c -> p j c", j=PACK))
+            if name == "w4":
+                dealt = rows.rearrange("(c t i) n -> t c i n", t=PACK, i=PACK)
+                for t in range(PACK):
+                    nc.sync.dma_start(out=raw[name, g][:, t, :], in_=dealt[t])
+            else:
+                nc.sync.dma_start(out=raw[name, g][:], in_=rows.rearrange("(p j) c -> p j c", j=PACK))
 
         load_words(0)
         load_scales(0)
@@ -88,18 +96,35 @@ def tile_picked_yfastf_none_po_kernel(
 
         def cast_weight(name, g, u):
             rounded[name, g, u] = sbuf(f"rounded_{name}_{g}_{u}", [P, 2 * P * PACK], BF16)
-            dst = rounded[name, g, u][:].rearrange("p (t m j) -> p m t j", t=2, j=PACK)
-            src = raw[name, g][:].rearrange("p j (m t) -> p m t j", t=PACK)[:, :, 2 * u : 2 * u + 2, :]
+            dst = rounded[name, g, u][:].rearrange("p (t c i j) -> p t c j i", t=2, i=PACK, j=PACK)
+            src = raw[name, g][:].rearrange("p j (c t i) -> p t c j i", t=PACK, i=PACK)[:, 2 * u : 2 * u + 2]
             where = CAST_ON[name][2 * g + u]
             if where == "s":
                 nc.scalar.copy(out=dst, in_=src)
             elif where == "v":
                 nc.vector.tensor_copy(out=dst, in_=src)
             else:
-                nc.gpsimd.tensor_scalar(out=dst, in0=src, scalar1=1.0, scalar2=0.0, op0=ALU.mult, op1=ALU.add)
+                for t in range(2):
+                    nc.gpsimd.tensor_scalar(
+                        out=dst[:, t].rearrange("p c j i -> p c i j"), in0=src[:, t].rearrange("p c j i -> p c i j"), scalar1=1.0, scalar2=0.0, op0=ALU.mult, op1=ALU.add
+                    )
+
+        def cast_last_weight():
+            whole = sbuf("rounded_w4", [P, PACK * P * PACK], BF16)
+            nc.scalar.copy(
+                out=whole[:].rearrange("p (t m j) -> p m j t", t=PACK, j=PACK),
+                in_=raw["w4", 0][:].rearrange("p j (m t) -> p m j t", t=PACK),
+            )
+            for u in range(2):
+                rounded["w4", 0, u] = whole[:, u * 2 * P * PACK : (u + 1) * 2 * P * PACK]
 
         def quantise_weight(name, g, u):
-            w_codes[name, g, u] = sbuf(f"codes_{name}_{g}_{u}", [P, 2 * P], U32)
+            if (name, g) == ("w1", 0):
+                w_codes[name, g, u] = reuse.tile(
+                    [P, 2 * P], U32, name=f"codes_{name}_{g}_{u}", offset=u * 2 * P * 4, align_bytes=64
+                )
+            else:
+                w_codes[name, g, u] = sbuf(f"codes_{name}_{g}_{u}", [P, 2 * P], U32)
             w_scales[name, g, u] = sbuf(f"scales_{name}_{g}_{u}", [P, 2 * P], U8)
             nc.vector.quantize_mx(
                 out=w_codes[name, g, u][:].bitcast(FP8X4), scales=w_scales[name, g, u][:], in_=rounded[name, g, u][:]
@@ -143,7 +168,8 @@ def tile_picked_yfastf_none_po_kernel(
                 cast_weight("w1", g, u)
             for u in range(2):
                 quantise_weight("w1", g, u)
-            for t in range(PACK):
+        for t in range(PACK):
+            for g in range(PASSES):
                 project_wide("w1", g, t)
 
         neg_y = [sbuf(f"neg_y{t}", [P, S], F32) for t in range(PACK)]
@@ -187,41 +213,51 @@ def tile_picked_yfastf_none_po_kernel(
                 accum_out=part[:, h, t : t + 1],
             )
 
+        def normalise(t):
+            nc.vector.reciprocal(out=inverse[t][:], in_=total[t][:])
+
+        def weigh_both(t):
+            normalise(t)
+            for h in range(HALVES):
+                weigh(t, h)
+
         for u in range(2):
             cast_weight("w2", 0, u)
-        for u in range(2):
-            for h in range(HALVES):
-                for t in (2 * u, 2 * u + 1):
-                    negate_and_min(t, h)
+        for h in range(HALVES):
+            for t in (0, 1):
+                negate_and_min(t, h)
         exponentiate(0)
+        quantise_weight("w2", 0, 0)
         for u in range(2):
             cast_weight("w2", 1, u)
-        for t in range(1, PACK):
-            exponentiate(t)
-        for u in range(2):
-            for g in range(PASSES):
-                quantise_weight("w2", g, u)
-        for t in range(PACK):
-            nc.vector.reciprocal(out=inverse[t][:], in_=total[t][:])
+        exponentiate(1)
+        for t in (2, 3):
+            negate_and_min(t, 0)
+        quantise_weight("w2", 1, 0)
+        for t in (2, 3):
+            negate_and_min(t, 1)
+        for g in range(PASSES):
+            quantise_weight("w2", g, 1)
         for t in range(PACK):
             for g in range(PASSES):
                 project_wide("w2", g, t)
+        cast_weight("w3", 0, 0)
+        exponentiate(2)
+        cast_weight("w3", 0, 1)
+        exponentiate(3)
+        cast_last_weight()
+        weigh_both(0)
+        cast_weight("w3", 1, 0)
+        weigh_both(1)
+        cast_weight("w3", 1, 1)
         for g in range(PASSES):
             for u in range(2):
-                cast_weight("w3", g, u)
-        for t in range(PACK):
-            for h in range(HALVES):
-                weigh(t, h)
-            if t >= 2:
-                for u in range(2):
-                    quantise_weight("w3", t - 2, u)
-        for u in range(2):
-            cast_weight("w4", 0, u)
+                quantise_weight("w3", g, u)
+        weigh_both(2)
+        weigh_both(3)
         nc.vector.tensor_tensor(out=gg[:], in0=part[:, 0, :], in1=part[:, 1, :], op=ALU.add)
-        for u in range(2):
-            quantise_weight("w4", 0, u)
 
-        for c in range(CHUNKS):
+        def hidden(c):
             for t in range(PACK):
                 for g in range(PASSES):
                     project(banks[c][:, t * CHUNK : (t + 1) * CHUNK], "w3", g, t, slice(c * CHUNK, (c + 1) * CHUNK))
@@ -230,7 +266,8 @@ def tile_picked_yfastf_none_po_kernel(
         z_codes = [sbuf(f"z_codes{c}", [P, CHUNK], U32) for c in range(CHUNKS)]
         z_scales = [sbuf(f"z_scales{c}", [P, CHUNK], U8) for c in range(CHUNKS)]
         result = [sbuf(f"result{c}", [P, PACK, 2 * CHUNK], F32) for c in range(CHUNKS // 2)]
-        result_bf = [sbuf(f"result_bf{c}", [P, CHUNK * PACK], BF16) for c in range(CHUNKS)]
+        pair_bf = [sbuf(f"pair_bf{c}", [P, 2 * CHUNK * PACK], BF16) for c in range(CHUNKS // 2)]
+        result_bf = [pair_bf[c // 2][:, (c % 2) * CHUNK * PACK : (c % 2 + 1) * CHUNK * PACK] for c in range(CHUNKS)]
         out_codes = sbuf("out_codes", [P, S], U32)
         out_scales = sbuf("out_scales", [P, S], U8)
         out_rows = out_0.rearrange("(p t) j -> p t j", t=PACK)
@@ -261,25 +298,36 @@ def tile_picked_yfastf_none_po_kernel(
         def leave_psum(c):
             mine = result[c // 2][:, :, (c % 2) * CHUNK : (c % 2 + 1) * CHUNK]
             nc.scalar.copy(out=mine, in_=banks[c][:].rearrange("p (t n) -> p t n", t=PACK))
-            dst = result_bf[c][:].rearrange("p (n t) -> p n t", t=PACK)
+            dst = result_bf[c].rearrange("p (n t) -> p n t", t=PACK)
             if c >= ROUND_ON_VECTOR_FROM:
-                nc.vector.tensor_copy(out=dst, in_=mine.rearrange("p t n -> p n t"))
+                nc.vector.tensor_copy(
+                    out=result_bf[c].rearrange("p (c i t) -> p c t i", i=PACK, t=PACK),
+                    in_=mine.rearrange("p t (c i) -> p c t i", i=PACK),
+                )
             else:
                 nc.scalar.copy(out=dst, in_=banks[c][:].rearrange("p (t n) -> p n t", t=PACK))
 
         def hand_out(c):
-            cols = slice(c * CHUNK, (c + 1) * CHUNK)
-            nc.vector.quantize_mx(out=out_codes[:, cols].bitcast(FP8X4), scales=out_scales[:, cols], in_=result_bf[c][:])
             if c % 2 == 1:
                 pair = slice((c - 1) * CHUNK, (c + 1) * CHUNK)
+                nc.vector.quantize_mx(
+                    out=out_codes[:, pair].bitcast(FP8X4), scales=out_scales[:, pair], in_=pair_bf[c // 2][:]
+                )
                 nc.sync.dma_start(out=out_rows[:, :, pair], in_=result[c // 2][:])
                 nc.sync.dma_start(out=out_words[:, pair], in_=out_codes[:, pair].bitcast(I32))
 
+        for c in range(HIDDEN_AHEAD):
+            hidden(c)
         for step in range(CHUNKS + 3):
             if step < CHUNKS:
                 scale_hidden(step)
+            if step == 0:
+                for u in range(2):
+                    quantise_weight("w4", 0, u)
             if 0 <= step - 1 < CHUNKS:
                 output_layer(step - 1)
+            if step + HIDDEN_AHEAD < CHUNKS:
+                hidden(step + HIDDEN_AHEAD)
             if 0 <= step - 2 < CHUNKS:
                 leave_psum(step - 2)
             if 0 <= step - 3 < CHUNKS:

@@ -17,16 +17,19 @@ ACT = mybir.ActivationFunctionType
 
 P = 128
 PACK = 4
+QUADRANT = 32
 K_PASS = P * PACK
 PASSES = K // K_PASS
 BANK = 512
 HALVES = S // BANK
-CHUNK = 128
+PAIR = 2
+CHUNK = BANK // PACK
 CHUNKS = S // CHUNK
-CAST_ON = {"w1": "ssvs", "w2": "ssvs", "w3": "ssvv"}
-HIDDEN_AHEAD = 3
-W3_AFTER = 1
-ROUND_ON_VECTOR_FROM = 3
+PER_LIST_COLUMN = 16
+PLACE_BYTES = 4 * PACK * N
+PLACE = {("w1", 0): 4, ("w1", 1): 0, ("w2", 0): 1, ("w2", 1): 2, ("w3", 0): 3, ("w3", 1): 0, ("w4", 0): 1}
+HIDDEN_AHEAD = 4
+SCALAR_ROUNDS = 3
 
 
 def tile_picked_yfastf_none_po_kernel(
@@ -35,113 +38,117 @@ def tile_picked_yfastf_none_po_kernel(
     nc = tc.nc
     with ExitStack() as ctx:
         keep = ctx.enter_context(tc.tile_pool(name="keep", bufs=1))
-        late = ctx.enter_context(tc.tile_pool(name="late", bufs=1))
-        reuse = ctx.enter_context(tc.tile_pool(name="reuse", bufs=1))
+        staging = ctx.enter_context(tc.tile_pool(name="staging", bufs=1))
+        shared = ctx.enter_context(tc.tile_pool(name="shared", bufs=1))
         psum = ctx.enter_context(tc.psum_pool(name="psum", bufs=1))
-        banks = [psum.tile([P, BANK], F32, name=f"bank{b}") for b in range(8)]
+        banks = [psum.tile([P, BANK], F32, name=f"bank{b}") for b in range(PACK * HALVES)]
 
         def sbuf(name, shape, dtype):
             return keep.tile(shape, dtype, name=name, align_bytes=64)
 
-        offsets = keep.tile([P, S // 16], U16, name="offsets")
+        offsets = keep.tile([P, S // PER_LIST_COLUMN], U16, name="offsets")
         nc.sync.dma_start(offsets[:], offs)
 
-        scale_table = reuse.tile([P, T], U8, name="scale_table", offset=0, align_bytes=64)
+        scale_table = shared.tile([P, T], U8, name="scale_table", offset=0, align_bytes=64)
         nc.vector.memset(scale_table[:].bitcast(I32), 0)
 
-        warm = late.tile([P, T + 7 * PACK * N], F32, name="warm", offset=0)
-        nc.vector.memset(warm[:, 0:1], 0.0)
-        nc.scalar.activation(out=warm[:, 1:2], in_=warm[:, 0:1], func=ACT.Exp)
+        zero = staging.tile([P, PASSES * T], F32, name="zero", offset=0)
+        one = sbuf("one", [P, 1], F32)
+        nc.vector.memset(zero[:, 0:1], 0.0)
+        nc.scalar.activation(out=one[:], in_=zero[:, 0:1], func=ACT.Exp)
 
-        word_table = [sbuf("word_table0", [P, T], U32), late.tile([P, T], U32, name="word_table1", offset=0)]
+        word_table = [
+            staging.tile([P, T], U32, name=f"word_table{g}", offset=2 * PLACE_BYTES * g) for g in range(PASSES)
+        ]
         weights = {"w1": w1, "w2": w2, "w3": w3, "w4": w4}
         raw = {}
 
-        def load_words(g):
+        def load_weight(name, g):
+            raw[name, g] = staging.tile(
+                [P, PACK, N], F32, name=f"raw_{name}_{g}", offset=PLACE_BYTES * PLACE[name, g]
+            )
+            rows = weights[name][g * K_PASS : (g + 1) * K_PASS, :]
+            if name == "w4":
+                by_slot = rows.rearrange("(c t e) n -> t c e n", t=PACK, e=PACK)
+                for t in range(PACK):
+                    nc.sync.dma_start(out=raw[name, g][:, t, :], in_=by_slot[t])
+            else:
+                nc.sync.dma_start(out=raw[name, g][:], in_=rows.rearrange("(p j) c -> p j c", j=PACK))
+
+        load_weight("w1", 0)
+        for g in range(PASSES):
+            nc.sync.dma_start(out=scale_table[PACK * g : P : 8, :].bitcast(I32), in_=x_scales[g].bitcast(I32))
+        for g in range(PASSES):
             nc.sync.dma_start(
                 out=word_table[g][:].bitcast(I32),
                 in_=x_words[g].rearrange("p n t -> p (n t)").bitcast(I32),
             )
 
-        def load_scales(g):
-            for q in range(4):
-                nc.sync.dma_start(
-                    out=scale_table[32 * q + PACK * g : 32 * q + PACK * (g + 1), :].bitcast(I32),
-                    in_=x_scales[g, 4 * q : 4 * q + 4, :].bitcast(I32),
-                )
-
-        def load_weight(name, g):
-            place = 4 * (T + len(raw) * PACK * N)
-            raw[name, g] = late.tile([P, PACK, N], F32, name=f"raw_{name}_{g}", offset=place)
-            rows = weights[name][g * K_PASS : (g + 1) * K_PASS, :]
-            if name == "w4":
-                dealt = rows.rearrange("(c t i) n -> t c i n", t=PACK, i=PACK)
-                for t in range(PACK):
-                    nc.sync.dma_start(out=raw[name, g][:, t, :], in_=dealt[t])
-            else:
-                nc.sync.dma_start(out=raw[name, g][:], in_=rows.rearrange("(p j) c -> p j c", j=PACK))
-
-        load_words(0)
-        load_scales(0)
-        load_weight("w1", 0)
-        load_scales(1)
-        load_words(1)
-        load_weight("w1", 1)
-        for name in ("w2", "w3"):
-            for g in range(PASSES):
-                load_weight(name, g)
-        load_weight("w4", 0)
-
         rounded, w_codes, w_scales = {}, {}, {}
 
-        def cast_weight(name, g, u):
-            rounded[name, g, u] = sbuf(f"rounded_{name}_{g}_{u}", [P, 2 * P * PACK], BF16)
-            dst = rounded[name, g, u][:].rearrange("p (t c i j) -> p t c j i", t=2, i=PACK, j=PACK)
-            src = raw[name, g][:].rearrange("p j (c t i) -> p t c j i", t=PACK, i=PACK)[:, 2 * u : 2 * u + 2]
-            where = CAST_ON[name][2 * g + u]
-            if where == "s":
+        def round_pair(name, g, u, engine):
+            rounded[name, g, u] = sbuf(f"rounded_{name}_{g}_{u}", [P, PAIR * P * PACK], BF16)
+            dst = rounded[name, g, u][:].rearrange("p (t c e j) -> p t c j e", t=PAIR, e=PACK, j=PACK)
+            src = raw[name, g][:].rearrange("p j (c t e) -> p t c j e", t=PACK, e=PACK)[:, PAIR * u : PAIR * (u + 1)]
+            if engine is nc.scalar:
                 nc.scalar.copy(out=dst, in_=src)
-            elif where == "v":
-                nc.vector.tensor_copy(out=dst, in_=src)
+            elif engine is nc.vector:
+                for t in range(PAIR):
+                    nc.vector.tensor_copy(out=dst[:, t], in_=src[:, t])
             else:
-                for t in range(2):
+                for t in range(PAIR):
                     nc.gpsimd.tensor_scalar(
-                        out=dst[:, t].rearrange("p c j i -> p c i j"), in0=src[:, t].rearrange("p c j i -> p c i j"), scalar1=1.0, scalar2=0.0, op0=ALU.mult, op1=ALU.add
+                        out=dst[:, t].rearrange("p c j e -> p c e j"),
+                        in0=src[:, t].rearrange("p c j e -> p c e j"),
+                        scalar1=1.0,
+                        scalar2=0.0,
+                        op0=ALU.mult,
+                        op1=ALU.add,
                     )
 
-        def cast_last_weight():
-            whole = sbuf("rounded_w4", [P, PACK * P * PACK], BF16)
-            nc.scalar.copy(
-                out=whole[:].rearrange("p (t m j) -> p m j t", t=PACK, j=PACK),
-                in_=raw["w4", 0][:].rearrange("p j (m t) -> p m j t", t=PACK),
-            )
-            for u in range(2):
-                rounded["w4", 0, u] = whole[:, u * 2 * P * PACK : (u + 1) * 2 * P * PACK]
+        def round_pass(name, g, engines):
+            for u, engine in enumerate(engines):
+                round_pair(name, g, u, engine)
 
-        def quantise_weight(name, g, u):
+        def round_w4():
+            for u in range(PACK // PAIR):
+                rounded["w4", 0, u] = sbuf(f"rounded_w4_{u}", [P, PAIR * P * PACK], BF16)
+                nc.scalar.copy(
+                    out=rounded["w4", 0, u][:].rearrange("p (t m j) -> p m j t", t=PAIR, j=PACK),
+                    in_=raw["w4", 0][:].rearrange("p j (m t) -> p m j t", t=PACK)[:, :, :, PAIR * u : PAIR * (u + 1)],
+                )
+
+        def quantise_pair(name, g, u, calls=1):
             if (name, g) == ("w1", 0):
-                w_codes[name, g, u] = reuse.tile(
-                    [P, 2 * P], U32, name=f"codes_{name}_{g}_{u}", offset=u * 2 * P * 4, align_bytes=64
+                w_codes[name, g, u] = shared.tile(
+                    [P, PAIR * P], U32, name=f"codes_{name}_{g}_{u}", offset=u * PAIR * P * 4, align_bytes=64
                 )
             else:
-                w_codes[name, g, u] = sbuf(f"codes_{name}_{g}_{u}", [P, 2 * P], U32)
-            w_scales[name, g, u] = sbuf(f"scales_{name}_{g}_{u}", [P, 2 * P], U8)
-            nc.vector.quantize_mx(
-                out=w_codes[name, g, u][:].bitcast(FP8X4), scales=w_scales[name, g, u][:], in_=rounded[name, g, u][:]
-            )
+                w_codes[name, g, u] = sbuf(f"codes_{name}_{g}_{u}", [P, PAIR * P], U32)
+            w_scales[name, g, u] = sbuf(f"scales_{name}_{g}_{u}", [P, PAIR * P], U8)
+            width = PAIR * P // calls
+            for n in range(calls):
+                cols = slice(n * width, (n + 1) * width)
+                nc.vector.quantize_mx(
+                    out=w_codes[name, g, u][:, cols].bitcast(FP8X4),
+                    scales=w_scales[name, g, u][:, cols],
+                    in_=rounded[name, g, u][:, PACK * n * width : PACK * (n + 1) * width],
+                )
 
         def stationary(name, g, t):
-            cols = slice((t % 2) * P, (t % 2 + 1) * P)
-            return w_codes[name, g, t // 2][:, cols].bitcast(FP8X4), w_scales[name, g, t // 2][:, cols]
+            cols = slice((t % PAIR) * P, (t % PAIR + 1) * P)
+            return w_codes[name, g, t // PAIR][:, cols].bitcast(FP8X4), w_scales[name, g, t // PAIR][:, cols]
 
         x_scale = sbuf("x_scale", [P, S], U8)
         x_codes = [sbuf(f"x_codes{g}", [P, S], U32) for g in range(PASSES)]
 
-        def gather_words(g, h):
-            nc.vector.tensor_copy(
-                out=x_codes[g][:, h * BANK : (h + 1) * BANK],
-                in_=word_table[g][:].indirect(offsets[:, h * BANK // 16 : (h + 1) * BANK // 16]),
-            )
+        def gather_words(g):
+            per_half = BANK // PER_LIST_COLUMN
+            for h in range(HALVES):
+                nc.vector.tensor_copy(
+                    out=x_codes[g][:, h * BANK : (h + 1) * BANK],
+                    in_=word_table[g][:].indirect(offsets[:, h * per_half : (h + 1) * per_half]),
+                )
 
         def project(out, name, g, t, cols):
             codes, scales = stationary(name, g, t)
@@ -155,22 +162,36 @@ def tile_picked_yfastf_none_po_kernel(
                 stop=(g == PASSES - 1),
             )
 
-        def project_wide(name, g, t):
-            for h in range(HALVES):
-                project(banks[HALVES * t + h][:], name, g, t, slice(h * BANK, (h + 1) * BANK))
+        def project_slots(name, slots):
+            for t in slots:
+                for g in range(PASSES):
+                    for h in range(HALVES):
+                        project(banks[HALVES * t + h][:], name, g, t, slice(h * BANK, (h + 1) * BANK))
 
+        picked_scale = sbuf("picked_scale", [P, S], U8)
+        nc.vector.tensor_copy(out=picked_scale[:], in_=scale_table[:].indirect(offsets[:]))
+        nc.vector.tensor_copy(out=x_scale[:].bitcast(I32), in_=picked_scale[:].bitcast(I32))
         for g in range(PASSES):
-            for h in range(HALVES):
-                gather_words(g, h)
-            if g == 0:
-                nc.vector.tensor_copy(out=x_scale[:], in_=scale_table[:].indirect(offsets[:]))
-            for u in range(2):
-                cast_weight("w1", g, u)
-            for u in range(2):
-                quantise_weight("w1", g, u)
-        for t in range(PACK):
-            for g in range(PASSES):
-                project_wide("w1", g, t)
+            for r in range(1, PACK):
+                nc.scalar.dma_start(
+                    out=x_scale[PACK * g + r : P : QUADRANT, :].bitcast(I32),
+                    in_=picked_scale[PACK * g + 8 * r : P : QUADRANT, :].bitcast(I32),
+                )
+
+        round_pass("w1", 0, (nc.scalar, nc.scalar))
+        for u in range(PACK // PAIR):
+            quantise_pair("w1", 0, u)
+        gather_words(0)
+        load_weight("w1", 1)
+        load_weight("w2", 0)
+        gather_words(1)
+        load_weight("w2", 1)
+        load_weight("w3", 0)
+        round_pass("w1", 1, (nc.vector, nc.scalar))
+        load_weight("w3", 1)
+        quantise_pair("w1", 1, 0, calls=PAIR)
+        quantise_pair("w1", 1, 1)
+        project_slots("w1", range(PACK))
 
         neg_y = [sbuf(f"neg_y{t}", [P, S], F32) for t in range(PACK)]
         ex = [sbuf(f"ex{t}", [P, S], F32) for t in range(PACK)]
@@ -201,6 +222,9 @@ def tile_picked_yfastf_none_po_kernel(
                 accum_out=total[t][:],
             )
 
+        def invert_total(t):
+            nc.vector.reciprocal(out=inverse[t][:], in_=total[t][:])
+
         def weigh(t, h):
             cols = slice(h * BANK, (h + 1) * BANK)
             nc.vector.scalar_tensor_tensor(
@@ -213,65 +237,70 @@ def tile_picked_yfastf_none_po_kernel(
                 accum_out=part[:, h, t : t + 1],
             )
 
-        def normalise(t):
-            nc.vector.reciprocal(out=inverse[t][:], in_=total[t][:])
-
-        def weigh_both(t):
-            normalise(t)
+        def weigh_slot(t):
+            invert_total(t)
             for h in range(HALVES):
                 weigh(t, h)
 
-        for u in range(2):
-            cast_weight("w2", 0, u)
-        for h in range(HALVES):
-            for t in (0, 1):
-                negate_and_min(t, h)
-        exponentiate(0)
-        quantise_weight("w2", 0, 0)
-        for u in range(2):
-            cast_weight("w2", 1, u)
-        exponentiate(1)
-        for t in (2, 3):
-            negate_and_min(t, 0)
-        quantise_weight("w2", 1, 0)
-        for t in (2, 3):
-            negate_and_min(t, 1)
+        round_pass("w2", 0, (nc.scalar, nc.gpsimd))
+        load_weight("w4", 0)
+        round_pass("w2", 1, (nc.scalar, nc.gpsimd))
+        negate_and_min(0, 0)
+        negate_and_min(1, 0)
+        negate_and_min(0, 1)
+        quantise_pair("w2", 0, 0)
+        negate_and_min(1, 1)
+        negate_and_min(2, 0)
+        negate_and_min(3, 0)
+        quantise_pair("w2", 1, 0)
+        negate_and_min(2, 1)
+        negate_and_min(3, 1)
+        project_slots("w2", (0, 1))
+        for t in range(PACK - 1):
+            exponentiate(t)
         for g in range(PASSES):
-            quantise_weight("w2", g, 1)
-        for t in range(PACK):
+            round_pass("w3", g, (nc.scalar, nc.gpsimd))
+        exponentiate(PACK - 1)
+        round_w4()
+        invert_total(0)
+        weigh(0, 0)
+        for g in range(PASSES):
+            quantise_pair("w2", g, 1)
+        project_slots("w2", (2, 3))
+        weigh(0, 1)
+        weigh_slot(1)
+        for u in (1, 0):
             for g in range(PASSES):
-                project_wide("w2", g, t)
-        cast_weight("w3", 0, 0)
-        exponentiate(2)
-        cast_weight("w3", 0, 1)
-        exponentiate(3)
-        cast_last_weight()
-        weigh_both(0)
-        cast_weight("w3", 1, 0)
-        weigh_both(1)
-        cast_weight("w3", 1, 1)
-        for g in range(PASSES):
-            for u in range(2):
-                quantise_weight("w3", g, u)
-        weigh_both(2)
-        weigh_both(3)
-        nc.vector.tensor_tensor(out=gg[:], in0=part[:, 0, :], in1=part[:, 1, :], op=ALU.add)
-
-        def hidden(c):
-            for t in range(PACK):
-                for g in range(PASSES):
-                    project(banks[c][:, t * CHUNK : (t + 1) * CHUNK], "w3", g, t, slice(c * CHUNK, (c + 1) * CHUNK))
+                quantise_pair("w3", g, u)
+        weigh_slot(2)
+        weigh_slot(3)
+        nc.vector.scalar_tensor_tensor(
+            out=gg[:], in0=part[:, 0, :], scalar=one[:], in1=part[:, 1, :], op0=ALU.mult, op1=ALU.add
+        )
 
         z = [sbuf(f"z{c}", [P, CHUNK * PACK], BF16) for c in range(CHUNKS)]
         z_codes = [sbuf(f"z_codes{c}", [P, CHUNK], U32) for c in range(CHUNKS)]
         z_scales = [sbuf(f"z_scales{c}", [P, CHUNK], U8) for c in range(CHUNKS)]
-        result = [sbuf(f"result{c}", [P, PACK, 2 * CHUNK], F32) for c in range(CHUNKS // 2)]
-        pair_bf = [sbuf(f"pair_bf{c}", [P, 2 * CHUNK * PACK], BF16) for c in range(CHUNKS // 2)]
-        result_bf = [pair_bf[c // 2][:, (c % 2) * CHUNK * PACK : (c % 2 + 1) * CHUNK * PACK] for c in range(CHUNKS)]
+        result = [sbuf(f"result{d}", [P, PACK, 2 * CHUNK], F32) for d in range(CHUNKS // 2)]
+        result_bf = [sbuf(f"result_bf{d}", [P, 2 * CHUNK * PACK], BF16) for d in range(CHUNKS // 2)]
         out_codes = sbuf("out_codes", [P, S], U32)
         out_scales = sbuf("out_scales", [P, S], U8)
         out_rows = out_0.rearrange("(p t) j -> p t j", t=PACK)
         out_words = out_1[0].rearrange("p n t -> p (n t)").bitcast(I32)
+
+        def tokens(first, last):
+            return slice(first * CHUNK, (last + 1) * CHUNK)
+
+        def result_of(c):
+            return result[c // 2][:, :, tokens(c % 2, c % 2)]
+
+        def result_bf_of(c):
+            return result_bf[c // 2][:, (c % 2) * CHUNK * PACK : (c % 2 + 1) * CHUNK * PACK]
+
+        def hidden(c):
+            for t in range(PACK):
+                for g in range(PASSES):
+                    project(banks[c][:, t * CHUNK : (t + 1) * CHUNK], "w3", g, t, tokens(c, c))
 
         def scale_hidden(c):
             nc.vector.tensor_tensor(
@@ -281,8 +310,10 @@ def tile_picked_yfastf_none_po_kernel(
                 op=ALU.mult,
             )
 
-        def output_layer(c):
+        def quantise_hidden(c):
             nc.vector.quantize_mx(out=z_codes[c][:].bitcast(FP8X4), scales=z_scales[c][:], in_=z[c][:])
+
+        def output_layer(c):
             for t in range(PACK):
                 codes, scales = stationary("w4", 0, t)
                 nc.tensor.matmul_mx(
@@ -296,45 +327,59 @@ def tile_picked_yfastf_none_po_kernel(
                 )
 
         def leave_psum(c):
-            mine = result[c // 2][:, :, (c % 2) * CHUNK : (c % 2 + 1) * CHUNK]
-            nc.scalar.copy(out=mine, in_=banks[c][:].rearrange("p (t n) -> p t n", t=PACK))
-            dst = result_bf[c].rearrange("p (n t) -> p n t", t=PACK)
-            if c >= ROUND_ON_VECTOR_FROM:
-                nc.vector.tensor_copy(
-                    out=result_bf[c].rearrange("p (c i t) -> p c t i", i=PACK, t=PACK),
-                    in_=mine.rearrange("p t (c i) -> p c t i", i=PACK),
+            nc.scalar.copy(out=result_of(c), in_=banks[c][:].rearrange("p (t n) -> p t n", t=PACK))
+            if c // 2 == CHUNKS // 2 - 1:
+                nc.sync.dma_start(out=out_rows[:, :, tokens(c, c)], in_=result_of(c))
+            elif c % 2 == 1:
+                nc.sync.dma_start(out=out_rows[:, :, tokens(c - 1, c)], in_=result[c // 2][:])
+            if c < SCALAR_ROUNDS:
+                nc.scalar.copy(
+                    out=result_bf_of(c).rearrange("p (n t) -> p n t", t=PACK),
+                    in_=banks[c][:].rearrange("p (t n) -> p n t", t=PACK),
                 )
-            else:
-                nc.scalar.copy(out=dst, in_=banks[c][:].rearrange("p (t n) -> p n t", t=PACK))
 
-        def hand_out(c):
-            if c % 2 == 1:
-                pair = slice((c - 1) * CHUNK, (c + 1) * CHUNK)
-                nc.vector.quantize_mx(
-                    out=out_codes[:, pair].bitcast(FP8X4), scales=out_scales[:, pair], in_=pair_bf[c // 2][:]
+        def quantise_result(c):
+            if c >= SCALAR_ROUNDS:
+                nc.vector.tensor_copy(
+                    out=result_bf_of(c).rearrange("p (a e t) -> p a t e", e=PACK, t=PACK),
+                    in_=result_of(c).rearrange("p t (a e) -> p a t e", e=PACK),
                 )
-                nc.sync.dma_start(out=out_rows[:, :, pair], in_=result[c // 2][:])
-                nc.sync.dma_start(out=out_words[:, pair], in_=out_codes[:, pair].bitcast(I32))
+            if c % 2 == 1:
+                cols = tokens(c - 1, c)
+                nc.vector.quantize_mx(
+                    out=out_codes[:, cols].bitcast(FP8X4), scales=out_scales[:, cols], in_=result_bf[c // 2][:]
+                )
+
+        def store_words(first, last):
+            cols = tokens(first, last)
+            nc.sync.dma_start(out=out_words[:, cols], in_=out_codes[:, cols].bitcast(I32))
 
         for c in range(HIDDEN_AHEAD):
             hidden(c)
-        for step in range(CHUNKS + 3):
+        for step in range(CHUNKS + 2):
             if step < CHUNKS:
                 scale_hidden(step)
             if step == 0:
-                for u in range(2):
-                    quantise_weight("w4", 0, u)
-            if 0 <= step - 1 < CHUNKS:
+                quantise_pair("w4", 0, 0)
+                quantise_hidden(0)
+                quantise_pair("w4", 0, 1)
+            if 1 < step <= CHUNKS:
+                quantise_hidden(step - 1)
+            if 1 <= step <= CHUNKS:
                 output_layer(step - 1)
             if step + HIDDEN_AHEAD < CHUNKS:
                 hidden(step + HIDDEN_AHEAD)
-            if 0 <= step - 2 < CHUNKS:
+            if step >= 2:
                 leave_psum(step - 2)
-            if 0 <= step - 3 < CHUNKS:
-                hand_out(step - 3)
-        for q in range(4):
+        for c in range(CHUNKS - 2):
+            quantise_result(c)
+        store_words(0, CHUNKS - 3)
+        for c in range(CHUNKS - 2, CHUNKS):
+            quantise_result(c)
+        store_words(CHUNKS - 2, CHUNKS - 1)
+        for q in range(P // QUADRANT):
             queue = nc.scalar if q % 2 else nc.sync
             queue.dma_start(
-                out=out_2[0, 4 * q : 4 * q + 4, :].bitcast(I32),
-                in_=out_scales[32 * q : 32 * q + 4, :].bitcast(I32),
+                out=out_2[0, PACK * q : PACK * (q + 1), :].bitcast(I32),
+                in_=out_scales[QUADRANT * q : QUADRANT * q + PACK, :].bitcast(I32),
             )

from contextlib import ExitStack

import concourse.mybir as mybir

K, T, S, H, N = 1024, 4096, 1024, 512, 512
FLOPS = 2 * S * (3 * K * N + H * N)

F32 = mybir.dt.float32
BF16 = mybir.dt.bfloat16
I32 = mybir.dt.int32
U32 = mybir.dt.uint32
U16 = mybir.dt.uint16
U8 = mybir.dt.uint8
FP8X4 = mybir.dt.float8_e4m3fn_x4
ALU = mybir.AluOpType
ACT = mybir.ActivationFunctionType

P = 128
PACK = 4
QUADRANT = 32
K_PASS = P * PACK
PASSES = K // K_PASS
BANK = 512
HALVES = S // BANK
PAIR = 2
CHUNK = BANK // PACK
CHUNKS = S // CHUNK
PER_LIST_COLUMN = 16
PLACE_BYTES = 4 * PACK * N
PLACE = {("w1", 0): 4, ("w1", 1): 0, ("w2", 0): 1, ("w2", 1): 2, ("w3", 0): 3, ("w3", 1): 0, ("w4", 0): 1}
HIDDEN_AHEAD = 4
SCALAR_ROUNDS = 3


def tile_picked_yfastf_none_po_kernel(
    tc, x_words, x_scales, w1, w2, w3, w4, offs, out_0, out_1, out_2
):
    nc = tc.nc
    with ExitStack() as ctx:
        keep = ctx.enter_context(tc.tile_pool(name="keep", bufs=1))
        staging = ctx.enter_context(tc.tile_pool(name="staging", bufs=1))
        shared = ctx.enter_context(tc.tile_pool(name="shared", bufs=1))
        psum = ctx.enter_context(tc.psum_pool(name="psum", bufs=1))
        banks = [psum.tile([P, BANK], F32, name=f"bank{b}") for b in range(PACK * HALVES)]

        def sbuf(name, shape, dtype):
            return keep.tile(shape, dtype, name=name, align_bytes=64)

        offsets = keep.tile([P, S // PER_LIST_COLUMN], U16, name="offsets")
        nc.sync.dma_start(offsets[:], offs)

        scale_table = shared.tile([P, T], U8, name="scale_table", offset=0, align_bytes=64)
        nc.vector.memset(scale_table[:].bitcast(I32), 0)

        zero = staging.tile([P, PASSES * T], F32, name="zero", offset=0)
        one = sbuf("one", [P, 1], F32)
        nc.vector.memset(zero[:, 0:1], 0.0)
        nc.scalar.activation(out=one[:], in_=zero[:, 0:1], func=ACT.Exp)

        word_table = [
            staging.tile([P, T], U32, name=f"word_table{g}", offset=2 * PLACE_BYTES * g) for g in range(PASSES)
        ]
        weights = {"w1": w1, "w2": w2, "w3": w3, "w4": w4}
        raw = {}

        def load_weight(name, g):
            raw[name, g] = staging.tile(
                [P, PACK, N], F32, name=f"raw_{name}_{g}", offset=PLACE_BYTES * PLACE[name, g]
            )
            rows = weights[name][g * K_PASS : (g + 1) * K_PASS, :]
            if name == "w4":
                by_slot = rows.rearrange("(c t e) n -> t c e n", t=PACK, e=PACK)
                for t in range(PACK):
                    nc.sync.dma_start(out=raw[name, g][:, t, :], in_=by_slot[t])
            else:
                nc.sync.dma_start(out=raw[name, g][:], in_=rows.rearrange("(p j) c -> p j c", j=PACK))

        load_weight("w1", 0)
        for g in range(PASSES):
            nc.sync.dma_start(out=scale_table[PACK * g : P : 8, :].bitcast(I32), in_=x_scales[g].bitcast(I32))
        for g in range(PASSES):
            nc.sync.dma_start(
                out=word_table[g][:].bitcast(I32),
                in_=x_words[g].rearrange("p n t -> p (n t)").bitcast(I32),
            )

        rounded, w_codes, w_scales = {}, {}, {}

        def round_pair(name, g, u, engine):
            rounded[name, g, u] = sbuf(f"rounded_{name}_{g}_{u}", [P, PAIR * P * PACK], BF16)
            dst = rounded[name, g, u][:].rearrange("p (t c e j) -> p t c j e", t=PAIR, e=PACK, j=PACK)
            src = raw[name, g][:].rearrange("p j (c t e) -> p t c j e", t=PACK, e=PACK)[:, PAIR * u : PAIR * (u + 1)]
            if engine is nc.scalar:
                nc.scalar.copy(out=dst, in_=src)
            elif engine is nc.vector:
                for t in range(PAIR):
                    nc.vector.tensor_copy(out=dst[:, t], in_=src[:, t])
            else:
                for t in range(PAIR):
                    nc.gpsimd.tensor_scalar(
                        out=dst[:, t].rearrange("p c j e -> p c e j"),
                        in0=src[:, t].rearrange("p c j e -> p c e j"),
                        scalar1=1.0,
                        scalar2=0.0,
                        op0=ALU.mult,
                        op1=ALU.add,
                    )

        def round_pass(name, g, engines):
            for u, engine in enumerate(engines):
                round_pair(name, g, u, engine)

        def round_w4():
            for u in range(PACK // PAIR):
                rounded["w4", 0, u] = sbuf(f"rounded_w4_{u}", [P, PAIR * P * PACK], BF16)
                nc.scalar.copy(
                    out=rounded["w4", 0, u][:].rearrange("p (t m j) -> p m j t", t=PAIR, j=PACK),
                    in_=raw["w4", 0][:].rearrange("p j (m t) -> p m j t", t=PACK)[:, :, :, PAIR * u : PAIR * (u + 1)],
                )

        def quantise_pair(name, g, u, calls=1):
            if (name, g) == ("w1", 0):
                w_codes[name, g, u] = shared.tile(
                    [P, PAIR * P], U32, name=f"codes_{name}_{g}_{u}", offset=u * PAIR * P * 4, align_bytes=64
                )
            else:
                w_codes[name, g, u] = sbuf(f"codes_{name}_{g}_{u}", [P, PAIR * P], U32)
            w_scales[name, g, u] = sbuf(f"scales_{name}_{g}_{u}", [P, PAIR * P], U8)
            width = PAIR * P // calls
            for n in range(calls):
                cols = slice(n * width, (n + 1) * width)
                nc.vector.quantize_mx(
                    out=w_codes[name, g, u][:, cols].bitcast(FP8X4),
                    scales=w_scales[name, g, u][:, cols],
                    in_=rounded[name, g, u][:, PACK * n * width : PACK * (n + 1) * width],
                )

        def stationary(name, g, t):
            cols = slice((t % PAIR) * P, (t % PAIR + 1) * P)
            return w_codes[name, g, t // PAIR][:, cols].bitcast(FP8X4), w_scales[name, g, t // PAIR][:, cols]

        x_scale = sbuf("x_scale", [P, S], U8)
        x_codes = [sbuf(f"x_codes{g}", [P, S], U32) for g in range(PASSES)]

        def gather_words(g):
            per_half = BANK // PER_LIST_COLUMN
            for h in range(HALVES):
                nc.vector.tensor_copy(
                    out=x_codes[g][:, h * BANK : (h + 1) * BANK],
                    in_=word_table[g][:].indirect(offsets[:, h * per_half : (h + 1) * per_half]),
                )

        def project(out, name, g, t, cols):
            codes, scales = stationary(name, g, t)
            nc.tensor.matmul_mx(
                out=out,
                lhsT=codes,
                lhsT_scale=scales,
                rhs=x_codes[g][:, cols].bitcast(FP8X4),
                rhs_scale=x_scale[PACK * g : P, cols],
                start=(g == 0),
                stop=(g == PASSES - 1),
            )

        def project_slots(name, slots):
            for t in slots:
                for g in range(PASSES):
                    for h in range(HALVES):
                        project(banks[HALVES * t + h][:], name, g, t, slice(h * BANK, (h + 1) * BANK))

        picked_scale = sbuf("picked_scale", [P, S], U8)
        nc.vector.tensor_copy(out=picked_scale[:], in_=scale_table[:].indirect(offsets[:]))
        nc.vector.tensor_copy(out=x_scale[:].bitcast(I32), in_=picked_scale[:].bitcast(I32))
        for g in range(PASSES):
            for r in range(1, PACK):
                nc.scalar.dma_start(
                    out=x_scale[PACK * g + r : P : QUADRANT, :].bitcast(I32),
                    in_=picked_scale[PACK * g + 8 * r : P : QUADRANT, :].bitcast(I32),
                )

        round_pass("w1", 0, (nc.scalar, nc.scalar))
        for u in range(PACK // PAIR):
            quantise_pair("w1", 0, u)
        gather_words(0)
        load_weight("w1", 1)
        load_weight("w2", 0)
        gather_words(1)
        load_weight("w2", 1)
        load_weight("w3", 0)
        round_pass("w1", 1, (nc.vector, nc.scalar))
        load_weight("w3", 1)
        quantise_pair("w1", 1, 0, calls=PAIR)
        quantise_pair("w1", 1, 1)
        project_slots("w1", range(PACK))

        neg_y = [sbuf(f"neg_y{t}", [P, S], F32) for t in range(PACK)]
        ex = [sbuf(f"ex{t}", [P, S], F32) for t in range(PACK)]
        neg_max = [sbuf(f"neg_max{t}", [P, HALVES], F32) for t in range(PACK)]
        total = [sbuf(f"total{t}", [P, 1], F32) for t in range(PACK)]
        inverse = [sbuf(f"inverse{t}", [P, 1], F32) for t in range(PACK)]
        part = sbuf("part", [P, HALVES, PACK], F32)
        gg = sbuf("gg", [P, PACK], F32)

        def negate_and_min(t, h):
            nc.vector.tensor_scalar(
                out=neg_y[t][:, h * BANK : (h + 1) * BANK],
                in0=banks[HALVES * t + h][:],
                scalar1=-1.0,
                scalar2=None if h == 0 else neg_max[t][:, h - 1 : h],
                op0=ALU.mult,
                op1=ALU.min,
                accum_out=neg_max[t][:, h : h + 1],
            )

        def exponentiate(t):
            nc.scalar.activation(
                out=ex[t][:],
                in_=neg_y[t][:],
                func=ACT.Exp,
                scale=-1.0,
                bias=neg_max[t][:, HALVES - 1 : HALVES],
                accum_out=total[t][:],
            )

        def invert_total(t):
            nc.vector.reciprocal(out=inverse[t][:], in_=total[t][:])

        def weigh(t, h):
            cols = slice(h * BANK, (h + 1) * BANK)
            nc.vector.scalar_tensor_tensor(
                out=neg_y[t][:, cols],
                in0=banks[HALVES * t + h][:],
                scalar=inverse[t][:],
                in1=ex[t][:, cols],
                op0=ALU.mult,
                op1=ALU.mult,
                accum_out=part[:, h, t : t + 1],
            )

        def weigh_slot(t):
            invert_total(t)
            for h in range(HALVES):
                weigh(t, h)

        round_pass("w2", 0, (nc.scalar, nc.gpsimd))
        load_weight("w4", 0)
        round_pass("w2", 1, (nc.scalar, nc.gpsimd))
        negate_and_min(0, 0)
        negate_and_min(1, 0)
        negate_and_min(0, 1)
        quantise_pair("w2", 0, 0)
        negate_and_min(1, 1)
        negate_and_min(2, 0)
        negate_and_min(3, 0)
        quantise_pair("w2", 1, 0)
        negate_and_min(2, 1)
        negate_and_min(3, 1)
        project_slots("w2", (0, 1))
        for t in range(PACK - 1):
            exponentiate(t)
        for g in range(PASSES):
            round_pass("w3", g, (nc.scalar, nc.gpsimd))
        exponentiate(PACK - 1)
        round_w4()
        invert_total(0)
        weigh(0, 0)
        for g in range(PASSES):
            quantise_pair("w2", g, 1)
        project_slots("w2", (2, 3))
        weigh(0, 1)
        weigh_slot(1)
        for u in (1, 0):
            for g in range(PASSES):
                quantise_pair("w3", g, u)
        weigh_slot(2)
        weigh_slot(3)
        nc.vector.scalar_tensor_tensor(
            out=gg[:], in0=part[:, 0, :], scalar=one[:], in1=part[:, 1, :], op0=ALU.mult, op1=ALU.add
        )

        z = [sbuf(f"z{c}", [P, CHUNK * PACK], BF16) for c in range(CHUNKS)]
        z_codes = [sbuf(f"z_codes{c}", [P, CHUNK], U32) for c in range(CHUNKS)]
        z_scales = [sbuf(f"z_scales{c}", [P, CHUNK], U8) for c in range(CHUNKS)]
        result = [sbuf(f"result{d}", [P, PACK, 2 * CHUNK], F32) for d in range(CHUNKS // 2)]
        result_bf = [sbuf(f"result_bf{d}", [P, 2 * CHUNK * PACK], BF16) for d in range(CHUNKS // 2)]
        out_codes = sbuf("out_codes", [P, S], U32)
        out_scales = sbuf("out_scales", [P, S], U8)
        out_rows = out_0.rearrange("(p t) j -> p t j", t=PACK)
        out_words = out_1[0].rearrange("p n t -> p (n t)").bitcast(I32)

        def tokens(first, last):
            return slice(first * CHUNK, (last + 1) * CHUNK)

        def result_of(c):
            return result[c // 2][:, :, tokens(c % 2, c % 2)]

        def result_bf_of(c):
            return result_bf[c // 2][:, (c % 2) * CHUNK * PACK : (c % 2 + 1) * CHUNK * PACK]

        def hidden(c):
            for t in range(PACK):
                for g in range(PASSES):
                    project(banks[c][:, t * CHUNK : (t + 1) * CHUNK], "w3", g, t, tokens(c, c))

        def scale_hidden(c):
            nc.vector.tensor_tensor(
                out=z[c][:].rearrange("p (n t) -> p n t", t=PACK),
                in0=banks[c][:].rearrange("p (t n) -> p n t", t=PACK),
                in1=gg[:].unsqueeze(1).to_broadcast([P, CHUNK, PACK]),
                op=ALU.mult,
            )

        def quantise_hidden(c):
            nc.vector.quantize_mx(out=z_codes[c][:].bitcast(FP8X4), scales=z_scales[c][:], in_=z[c][:])

        def output_layer(c):
            for t in range(PACK):
                codes, scales = stationary("w4", 0, t)
                nc.tensor.matmul_mx(
                    out=banks[c][:, t * CHUNK : (t + 1) * CHUNK],
                    lhsT=codes,
                    lhsT_scale=scales,
                    rhs=z_codes[c][:].bitcast(FP8X4),
                    rhs_scale=z_scales[c][:],
                    start=True,
                    stop=True,
                )

        def leave_psum(c):
            nc.scalar.copy(out=result_of(c), in_=banks[c][:].rearrange("p (t n) -> p t n", t=PACK))
            if c // 2 == CHUNKS // 2 - 1:
                nc.sync.dma_start(out=out_rows[:, :, tokens(c, c)], in_=result_of(c))
            elif c % 2 == 1:
                nc.sync.dma_start(out=out_rows[:, :, tokens(c - 1, c)], in_=result[c // 2][:])
            if c < SCALAR_ROUNDS:
                nc.scalar.copy(
                    out=result_bf_of(c).rearrange("p (n t) -> p n t", t=PACK),
                    in_=banks[c][:].rearrange("p (t n) -> p n t", t=PACK),
                )

        def quantise_result(c):
            if c >= SCALAR_ROUNDS:
                nc.vector.tensor_copy(
                    out=result_bf_of(c).rearrange("p (a e t) -> p a t e", e=PACK, t=PACK),
                    in_=result_of(c).rearrange("p t (a e) -> p a t e", e=PACK),
                )
            if c % 2 == 1:
                cols = tokens(c - 1, c)
                nc.vector.quantize_mx(
                    out=out_codes[:, cols].bitcast(FP8X4), scales=out_scales[:, cols], in_=result_bf[c // 2][:]
                )

        def store_words(first, last):
            cols = tokens(first, last)
            nc.sync.dma_start(out=out_words[:, cols], in_=out_codes[:, cols].bitcast(I32))

        for c in range(HIDDEN_AHEAD):
            hidden(c)
        for step in range(CHUNKS + 2):
            if step < CHUNKS:
                scale_hidden(step)
            if step == 0:
                quantise_pair("w4", 0, 0)
                quantise_hidden(0)
                quantise_pair("w4", 0, 1)
            if 1 < step <= CHUNKS:
                quantise_hidden(step - 1)
            if 1 <= step <= CHUNKS:
                output_layer(step - 1)
            if step + HIDDEN_AHEAD < CHUNKS:
                hidden(step + HIDDEN_AHEAD)
            if step >= 2:
                leave_psum(step - 2)
        for c in range(CHUNKS - 2):
            quantise_result(c)
        store_words(0, CHUNKS - 3)
        for c in range(CHUNKS - 2, CHUNKS):
            quantise_result(c)
        store_words(CHUNKS - 2, CHUNKS - 1)
        for q in range(P // QUADRANT):
            queue = nc.scalar if q % 2 else nc.sync
            queue.dma_start(
                out=out_2[0, PACK * q : PACK * (q + 1), :].bitcast(I32),
                in_=out_scales[QUADRANT * q : QUADRANT * q + PACK, :].bitcast(I32),
            )
